import numpy as np
import ml_dtypes


def mxq(x, axis, fmt="e4m3"):
    dtype, down = {"e4m3": (ml_dtypes.float8_e4m3fn, 7), "e5m2": (ml_dtypes.float8_e5m2, 14)}[fmt]
    v = np.moveaxis(np.asarray(x, np.float32).astype(ml_dtypes.bfloat16).astype(np.float64), axis, -1)
    blocks = v.reshape(v.shape[:-1] + (-1, 32))
    amax = np.abs(blocks).max(-1, keepdims=True)
    byte = np.maximum(np.where(amax > 0, np.frexp(amax)[1] - 1 + 127, 0) - down, 1)
    scale = np.exp2(byte - 127.0)
    codes = (blocks / scale).astype(np.float32).astype(dtype).astype(np.float64)
    return np.moveaxis((codes * scale).reshape(v.shape), -1, axis)


WIDE = False


def mx_kscale(k, group=512):
    if not WIDE:
        return np.ones(k)
    levels = np.array([18, -18])
    if group != 512:
        return np.exp2(np.random.permutation(np.resize(levels, k // group))).repeat(group)
    if k % 512:
        return np.exp2(np.random.permutation(np.resize(levels, k // 32))).repeat(32)
    a = np.empty((k // 512, 16))
    for p in range(k // 512):
        a[p, :8] = np.random.permutation(np.resize(levels, 8))
        for g in range(8):
            far = levels[np.abs(levels - a[p, g]) >= 10]
            a[p, g + 8] = far[np.random.randint(len(far))]
    return np.exp2(a.ravel()).repeat(32)


def f64(x):
    return np.asarray(x).astype(np.float64)


G, D, M, N = 8, 128, 128, 512


def setup_inputs():
    n = np.random.standard_normal
    s = mx_kscale(D, 0)[:, None]
    return {
        "x": (n((G, D, N)) * s).astype(np.float32),
        "w": (n((G, D, M)) / np.sqrt(D) / s).astype(np.float32),
        "b": (0.5 * n((G, M, 1))).astype(np.float32),
        "r": n((G, M, N)).astype(np.float32),
    }


def reference(x, w, b, r):
    xq = mxq(f64(x), 1, "e4m3")
    y = mxq(f64(w), 1, "e4m3").transpose(0, 2, 1) @ xq
    y = y + f64(b)
    y = 1.0 / (1.0 + np.exp(-(y)))
    y = y + f64(r)
    return y

@@ -1,0 +1,133 @@
+from contextlib import ExitStack
+
+import concourse.mybir as mybir
+
+G, D, M, N = 8, 128, 128, 512
+FLOPS = 2 * G * D * M * N
+
+F32 = mybir.dt.float32
+BF16 = mybir.dt.bfloat16
+U32 = mybir.dt.uint32
+U8 = mybir.dt.uint8
+FP8X4 = mybir.dt.float8_e4m3fn_x4
+SIGMOID = mybir.ActivationFunctionType.Sigmoid
+ADD = mybir.AluOpType.add
+
+P = 128
+PACK = 4
+ROWS = D // PACK
+SIDE = P // ROWS
+SETS = G // SIDE
+HALF = N // 2
+PAIR = 2
+
+
+def tile_rows_glin_sigmoid_bias_res_kernel(tc, x, w, b, r, out):
+    nc = tc.nc
+    with ExitStack() as ctx:
+        sb = ctx.enter_context(tc.tile_pool(name="sb", bufs=1))
+        ps = ctx.enter_context(tc.psum_pool(name="ps", bufs=1))
+        ctx.enter_context(tc.manual_schedule())
+
+        x_raw = [sb.tile([P, PACK, N], F32, name="x_raw%d" % s) for s in range(SETS)]
+        x_bf = [[sb.tile([P, HALF, PACK], BF16, name="x_bf%d_%d" % (s, h), align_bytes=64) for h in range(2)] for s in range(SETS)]
+        x_codes = [sb.tile([P, N], U32, name="x_codes%d" % s, align_bytes=64) for s in range(SETS)]
+        x_scales = [sb.tile([P, N], U8, name="x_scales%d" % s, align_bytes=64) for s in range(SETS)]
+        w_raw = sb.tile([P, SETS, PACK, M], F32, name="w_raw")
+        w_bf = [sb.tile([P, M, PACK], BF16, name="w_bf%d" % s, align_bytes=64) for s in range(SETS)]
+        w_codes = [sb.tile([P, M], U32, name="w_codes%d" % s, align_bytes=64) for s in range(SETS)]
+        w_scales = [sb.tile([P, M], U8, name="w_scales%d" % s, align_bytes=64) for s in range(SETS)]
+        b_rows = sb.tile([P, 32], F32, name="b_rows", align_bytes=64)
+        b_cols = sb.tile([P, 32], F32, name="b_cols", align_bytes=64)
+        warm = sb.tile([P, 8], F32, name="warm")
+        warm_out = sb.tile([P, 8], F32, name="warm_out")
+        res = [sb.tile([P, PAIR, N], F32, name="res%d" % i) for i in range(G // PAIR)]
+        act = [sb.tile([P, N], F32, name="act%d" % g) for g in range(G)]
+        y = [sb.tile([P, PAIR, N], F32, name="y%d" % i) for i in range(G // PAIR)]
+        acc = [ps.tile([P, N], F32, name="acc%d" % g) for g in range(G)]
+
+        x_rows = x.rearrange("g d n -> (g d) n").rearrange("(s p j) n -> s p j n", s=SETS, j=PACK)
+        w_rows = w.rearrange("g d m -> (g d) m").rearrange("(s p j) m -> p s j m", s=SETS, j=PACK)
+
+        nc.vector.memset(b_rows[:], 0.0)
+        nc.vector.memset(warm[:], 0.0)
+        nc.sync.dma_start(out=x_raw[0][:], in_=x_rows[0])
+        nc.sync.dma_start(out=b_rows[0:P:4, :], in_=b.rearrange("g (q i) o -> q g (i o)", q=4))
+        nc.sync.dma_start(out=w_raw[:], in_=w_rows)
+        nc.sync.dma_start(out=x_raw[1][:], in_=x_rows[1])
+        for i in range(G // PAIR):
+            nc.sync.dma_start(out=res[i][:], in_=r[PAIR * i : PAIR * (i + 1)].rearrange("g m n -> m g n"))
+
+        nc.scalar.activation(out=warm_out[:, 0:1], in_=warm[:, 0:1], func=SIGMOID)
+
+        def interleave_x(s, h):
+            src = x_raw[s][:, :, h * HALF : (h + 1) * HALF].rearrange("p j n -> p n j")
+            if h == 0:
+                nc.vector.tensor_copy(out=x_bf[s][h][:], in_=src)
+            else:
+                nc.scalar.copy(out=x_bf[s][h][:], in_=src)
+
+        def quantize_x(s, h):
+            cols = slice(h * HALF, (h + 1) * HALF)
+            nc.vector.quantize_mx(
+                out=x_codes[s][:, cols].bitcast(FP8X4),
+                scales=x_scales[s][:, cols],
+                in_=x_bf[s][h][:].rearrange("p n j -> p (n j)"),
+            )
+
+        def interleave_w(s):
+            src = w_raw[:, s].rearrange("p j m -> p m j")
+            if s == 0:
+                nc.vector.tensor_copy(out=w_bf[s][:], in_=src)
+            else:
+                nc.scalar.copy(out=w_bf[s][:], in_=src)
+
+        def quantize_w(s):
+            nc.vector.quantize_mx(
+                out=w_codes[s][:].bitcast(FP8X4),
+                scales=w_scales[s][:],
+                in_=w_bf[s][:].rearrange("p m j -> p (m j)"),
+            )
+
+        def multiply(s):
+            for c in range(SIDE):
+                rows = slice(ROWS * c, ROWS * (c + 1))
+                nc.tensor.matmul_mx(
+                    out=acc[SIDE * s + c][:],
+                    lhsT=w_codes[s][rows, :].bitcast(FP8X4),
+                    lhsT_scale=w_scales[s][rows, :],
+                    rhs=x_codes[s][rows, :].bitcast(FP8X4),
+                    rhs_scale=x_scales[s][rows, :],
+                    start=True,
+                    stop=True,
+                )
+
+        def activate(g):
+            nc.scalar.activation(out=act[g][:], in_=acc[g][:], func=SIGMOID, bias=b_cols[:, 4 * g : 4 * g + 1])
+
+        def finish(g):
+            i, e = divmod(g, PAIR)
+            nc.vector.tensor_tensor(out=y[i][:, e, :], in0=act[g][:], in1=res[i][:, e, :], op=ADD)
+            if e == PAIR - 1:
+                nc.sync.dma_start(out=out[PAIR * i : PAIR * (i + 1)].rearrange("g m n -> m g n"), in_=y[i][:])
+
+        interleave_x(0, 1)
+        interleave_x(0, 0)
+        nc.vector.transpose(out=b_cols[:], in_=b_rows[:])
+        quantize_x(0, 0)
+        interleave_w(0)
+        interleave_w(1)
+        quantize_x(0, 1)
+        quantize_w(0)
+        multiply(0)
+        quantize_w(1)
+        activate(0)
+        interleave_x(1, 1)
+        interleave_x(1, 0)
+        quantize_x(1, 0)
+        finish(0)
+        quantize_x(1, 1)
+        multiply(1)
+        for g in range(1, G):
+            activate(g)
+            finish(g)

@@ -18,8 +18,10 @@ PACK = 4
 ROWS = D // PACK
 SIDE = P // ROWS
 SETS = G // SIDE
-HALF = N // 2
+VEC_COLS = 352
+RUN = 2
 PAIR = 2
+STORES = ((0, 2), (2, 4), (4, 6), (6, 7), (7, 8))
 
 
 def tile_rows_glin_sigmoid_bias_res_kernel(tc, x, w, b, r, out):
@@ -30,7 +32,7 @@ def tile_rows_glin_sigmoid_bias_res_kernel(tc, x, w, b, r, out):
         ctx.enter_context(tc.manual_schedule())
 
         x_raw = [sb.tile([P, PACK, N], F32, name="x_raw%d" % s) for s in range(SETS)]
-        x_bf = [[sb.tile([P, HALF, PACK], BF16, name="x_bf%d_%d" % (s, h), align_bytes=64) for h in range(2)] for s in range(SETS)]
+        x_bf = [sb.tile([P, N, PACK], BF16, name="x_bf%d" % s, align_bytes=64) for s in range(SETS)]
         x_codes = [sb.tile([P, N], U32, name="x_codes%d" % s, align_bytes=64) for s in range(SETS)]
         x_scales = [sb.tile([P, N], U8, name="x_scales%d" % s, align_bytes=64) for s in range(SETS)]
         w_raw = sb.tile([P, SETS, PACK, M], F32, name="w_raw")
@@ -43,7 +45,7 @@ def tile_rows_glin_sigmoid_bias_res_kernel(tc, x, w, b, r, out):
         warm_out = sb.tile([P, 8], F32, name="warm_out")
         res = [sb.tile([P, PAIR, N], F32, name="res%d" % i) for i in range(G // PAIR)]
         act = [sb.tile([P, N], F32, name="act%d" % g) for g in range(G)]
-        y = [sb.tile([P, PAIR, N], F32, name="y%d" % i) for i in range(G // PAIR)]
+        y = {first: sb.tile([P, last - first, N], F32, name="y%d" % first) for first, last in STORES}
         acc = [ps.tile([P, N], F32, name="acc%d" % g) for g in range(G)]
 
         x_rows = x.rearrange("g d n -> (g d) n").rearrange("(s p j) n -> s p j n", s=SETS, j=PACK)
@@ -60,27 +62,22 @@ def tile_rows_glin_sigmoid_bias_res_kernel(tc, x, w, b, r, out):
 
         nc.scalar.activation(out=warm_out[:, 0:1], in_=warm[:, 0:1], func=SIGMOID)
 
-        def interleave_x(s, h):
-            src = x_raw[s][:, :, h * HALF : (h + 1) * HALF].rearrange("p j n -> p n j")
-            if h == 0:
-                nc.vector.tensor_copy(out=x_bf[s][h][:], in_=src)
-            else:
-                nc.scalar.copy(out=x_bf[s][h][:], in_=src)
-
-        def quantize_x(s, h):
-            cols = slice(h * HALF, (h + 1) * HALF)
-            nc.vector.quantize_mx(
-                out=x_codes[s][:, cols].bitcast(FP8X4),
-                scales=x_scales[s][:, cols],
-                in_=x_bf[s][h][:].rearrange("p n j -> p (n j)"),
+        def interleave(copy, dst, src):
+            copy(
+                out=dst.rearrange("p (c i) j -> p c j i", i=RUN),
+                in_=src.rearrange("p j (c i) -> p c j i", i=RUN),
             )
 
-        def interleave_w(s):
-            src = w_raw[:, s].rearrange("p j m -> p m j")
-            if s == 0:
-                nc.vector.tensor_copy(out=w_bf[s][:], in_=src)
-            else:
-                nc.scalar.copy(out=w_bf[s][:], in_=src)
+        def interleave_x(s):
+            interleave(nc.scalar.copy, x_bf[s][:, VEC_COLS:, :], x_raw[s][:, :, VEC_COLS:])
+            interleave(nc.vector.tensor_copy, x_bf[s][:, :VEC_COLS, :], x_raw[s][:, :, :VEC_COLS])
+
+        def quantize_x(s):
+            nc.vector.quantize_mx(
+                out=x_codes[s][:].bitcast(FP8X4),
+                scales=x_scales[s][:],
+                in_=x_bf[s][:].rearrange("p n j -> p (n j)"),
+            )
 
         def quantize_w(s):
             nc.vector.quantize_mx(
@@ -106,28 +103,22 @@ def tile_rows_glin_sigmoid_bias_res_kernel(tc, x, w, b, r, out):
             nc.scalar.activation(out=act[g][:], in_=acc[g][:], func=SIGMOID, bias=b_cols[:, 4 * g : 4 * g + 1])
 
         def finish(g):
-            i, e = divmod(g, PAIR)
-            nc.vector.tensor_tensor(out=y[i][:, e, :], in0=act[g][:], in1=res[i][:, e, :], op=ADD)
-            if e == PAIR - 1:
-                nc.sync.dma_start(out=out[PAIR * i : PAIR * (i + 1)].rearrange("g m n -> m g n"), in_=y[i][:])
+            first, last = [span for span in STORES if span[0] <= g < span[1]][0]
+            nc.vector.tensor_tensor(out=y[first][:, g - first, :], in0=act[g][:], in1=res[g // PAIR][:, g % PAIR, :], op=ADD)
+            if g == last - 1:
+                nc.sync.dma_start(out=out[first:last].rearrange("g m n -> m g n"), in_=y[first][:])
 
-        interleave_x(0, 1)
-        interleave_x(0, 0)
+        interleave_x(0)
         nc.vector.transpose(out=b_cols[:], in_=b_rows[:])
-        quantize_x(0, 0)
-        interleave_w(0)
-        interleave_w(1)
-        quantize_x(0, 1)
+        quantize_x(0)
+        interleave(nc.vector.tensor_copy, w_bf[0][:], w_raw[:, 0])
+        interleave(nc.scalar.copy, w_bf[1][:], w_raw[:, 1])
         quantize_w(0)
         multiply(0)
         quantize_w(1)
-        activate(0)
-        interleave_x(1, 1)
-        interleave_x(1, 0)
-        quantize_x(1, 0)
-        finish(0)
-        quantize_x(1, 1)
+        interleave_x(1)
+        quantize_x(1)
         multiply(1)
-        for g in range(1, G):
+        for g in range(G):
             activate(g)
             finish(g)

@@ -18,10 +18,10 @@ PACK = 4
 ROWS = D // PACK
 SIDE = P // ROWS
 SETS = G // SIDE
-VEC_COLS = 352
+VEC_COLS = (352, 336)
 RUN = 2
-PAIR = 2
-STORES = ((0, 2), (2, 4), (4, 6), (6, 7), (7, 8))
+LOADS = ((0, 2), (2, 4), (4, 6), (6, 8))
+STORES = ((0, 2), (2, 4), (4, 6), (6, 8))
 
 
 def tile_rows_glin_sigmoid_bias_res_kernel(tc, x, w, b, r, out):
@@ -35,7 +35,7 @@ def tile_rows_glin_sigmoid_bias_res_kernel(tc, x, w, b, r, out):
         x_bf = [sb.tile([P, N, PACK], BF16, name="x_bf%d" % s, align_bytes=64) for s in range(SETS)]
         x_codes = [sb.tile([P, N], U32, name="x_codes%d" % s, align_bytes=64) for s in range(SETS)]
         x_scales = [sb.tile([P, N], U8, name="x_scales%d" % s, align_bytes=64) for s in range(SETS)]
-        w_raw = sb.tile([P, SETS, PACK, M], F32, name="w_raw")
+        w_raw = [sb.tile([P, PACK, M], F32, name="w_raw%d" % s) for s in range(SETS)]
         w_bf = [sb.tile([P, M, PACK], BF16, name="w_bf%d" % s, align_bytes=64) for s in range(SETS)]
         w_codes = [sb.tile([P, M], U32, name="w_codes%d" % s, align_bytes=64) for s in range(SETS)]
         w_scales = [sb.tile([P, M], U8, name="w_scales%d" % s, align_bytes=64) for s in range(SETS)]
@@ -43,22 +43,23 @@ def tile_rows_glin_sigmoid_bias_res_kernel(tc, x, w, b, r, out):
         b_cols = sb.tile([P, 32], F32, name="b_cols", align_bytes=64)
         warm = sb.tile([P, 8], F32, name="warm")
         warm_out = sb.tile([P, 8], F32, name="warm_out")
-        res = [sb.tile([P, PAIR, N], F32, name="res%d" % i) for i in range(G // PAIR)]
+        res = {first: sb.tile([P, last - first, N], F32, name="res%d" % first) for first, last in LOADS}
         act = [sb.tile([P, N], F32, name="act%d" % g) for g in range(G)]
         y = {first: sb.tile([P, last - first, N], F32, name="y%d" % first) for first, last in STORES}
         acc = [ps.tile([P, N], F32, name="acc%d" % g) for g in range(G)]
 
         x_rows = x.rearrange("g d n -> (g d) n").rearrange("(s p j) n -> s p j n", s=SETS, j=PACK)
-        w_rows = w.rearrange("g d m -> (g d) m").rearrange("(s p j) m -> p s j m", s=SETS, j=PACK)
+        w_rows = w.rearrange("g d m -> (g d) m").rearrange("(s p j) m -> s p j m", s=SETS, j=PACK)
 
         nc.vector.memset(b_rows[:], 0.0)
         nc.vector.memset(warm[:], 0.0)
         nc.sync.dma_start(out=x_raw[0][:], in_=x_rows[0])
+        nc.sync.dma_start(out=w_raw[0][:], in_=w_rows[0])
         nc.sync.dma_start(out=b_rows[0:P:4, :], in_=b.rearrange("g (q i) o -> q g (i o)", q=4))
-        nc.sync.dma_start(out=w_raw[:], in_=w_rows)
         nc.sync.dma_start(out=x_raw[1][:], in_=x_rows[1])
-        for i in range(G // PAIR):
-            nc.sync.dma_start(out=res[i][:], in_=r[PAIR * i : PAIR * (i + 1)].rearrange("g m n -> m g n"))
+        nc.sync.dma_start(out=w_raw[1][:], in_=w_rows[1])
+        for first, last in LOADS:
+            nc.sync.dma_start(out=res[first][:], in_=r[first:last].rearrange("g m n -> m g n"))
 
         nc.scalar.activation(out=warm_out[:, 0:1], in_=warm[:, 0:1], func=SIGMOID)
 
@@ -69,8 +70,8 @@ def tile_rows_glin_sigmoid_bias_res_kernel(tc, x, w, b, r, out):
             )
 
         def interleave_x(s):
-            interleave(nc.scalar.copy, x_bf[s][:, VEC_COLS:, :], x_raw[s][:, :, VEC_COLS:])
-            interleave(nc.vector.tensor_copy, x_bf[s][:, :VEC_COLS, :], x_raw[s][:, :, :VEC_COLS])
+            interleave(nc.scalar.copy, x_bf[s][:, VEC_COLS[s] :, :], x_raw[s][:, :, VEC_COLS[s] :])
+            interleave(nc.vector.tensor_copy, x_bf[s][:, : VEC_COLS[s], :], x_raw[s][:, :, : VEC_COLS[s]])
 
         def quantize_x(s):
             nc.vector.quantize_mx(
@@ -104,21 +105,19 @@ def tile_rows_glin_sigmoid_bias_res_kernel(tc, x, w, b, r, out):
 
         def finish(g):
             first, last = [span for span in STORES if span[0] <= g < span[1]][0]
-            nc.vector.tensor_tensor(out=y[first][:, g - first, :], in0=act[g][:], in1=res[g // PAIR][:, g % PAIR, :], op=ADD)
+            start = [span[0] for span in LOADS if span[0] <= g < span[1]][0]
+            nc.vector.tensor_tensor(out=y[first][:, g - first, :], in0=act[g][:], in1=res[start][:, g - start, :], op=ADD)
             if g == last - 1:
                 nc.sync.dma_start(out=out[first:last].rearrange("g m n -> m g n"), in_=y[first][:])
 
-        interleave_x(0)
-        nc.vector.transpose(out=b_cols[:], in_=b_rows[:])
-        quantize_x(0)
-        interleave(nc.vector.tensor_copy, w_bf[0][:], w_raw[:, 0])
-        interleave(nc.scalar.copy, w_bf[1][:], w_raw[:, 1])
-        quantize_w(0)
-        multiply(0)
-        quantize_w(1)
-        interleave_x(1)
-        quantize_x(1)
-        multiply(1)
+        for s in range(SETS):
+            interleave_x(s)
+            interleave(nc.vector.tensor_copy, w_bf[s][:], w_raw[s][:])
+            quantize_x(s)
+            quantize_w(s)
+            multiply(s)
+            if s == 0:
+                nc.vector.transpose(out=b_cols[:], in_=b_rows[:])
         for g in range(G):
             activate(g)
             finish(g)

@@ -18,7 +18,6 @@ PACK = 4
 ROWS = D // PACK
 SIDE = P // ROWS
 SETS = G // SIDE
-VEC_COLS = (352, 336)
 RUN = 2
 LOADS = ((0, 2), (2, 4), (4, 6), (6, 8))
 STORES = ((0, 2), (2, 4), (4, 6), (6, 8))
@@ -41,8 +40,6 @@ def tile_rows_glin_sigmoid_bias_res_kernel(tc, x, w, b, r, out):
         w_scales = [sb.tile([P, M], U8, name="w_scales%d" % s, align_bytes=64) for s in range(SETS)]
         b_rows = sb.tile([P, 32], F32, name="b_rows", align_bytes=64)
         b_cols = sb.tile([P, 32], F32, name="b_cols", align_bytes=64)
-        warm = sb.tile([P, 8], F32, name="warm")
-        warm_out = sb.tile([P, 8], F32, name="warm_out")
         res = {first: sb.tile([P, last - first, N], F32, name="res%d" % first) for first, last in LOADS}
         act = [sb.tile([P, N], F32, name="act%d" % g) for g in range(G)]
         y = {first: sb.tile([P, last - first, N], F32, name="y%d" % first) for first, last in STORES}
@@ -52,7 +49,6 @@ def tile_rows_glin_sigmoid_bias_res_kernel(tc, x, w, b, r, out):
         w_rows = w.rearrange("g d m -> (g d) m").rearrange("(s p j) m -> s p j m", s=SETS, j=PACK)
 
         nc.vector.memset(b_rows[:], 0.0)
-        nc.vector.memset(warm[:], 0.0)
         nc.sync.dma_start(out=x_raw[0][:], in_=x_rows[0])
         nc.sync.dma_start(out=w_raw[0][:], in_=w_rows[0])
         nc.sync.dma_start(out=b_rows[0:P:4, :], in_=b.rearrange("g (q i) o -> q g (i o)", q=4))
@@ -61,17 +57,11 @@ def tile_rows_glin_sigmoid_bias_res_kernel(tc, x, w, b, r, out):
         for first, last in LOADS:
             nc.sync.dma_start(out=res[first][:], in_=r[first:last].rearrange("g m n -> m g n"))
 
-        nc.scalar.activation(out=warm_out[:, 0:1], in_=warm[:, 0:1], func=SIGMOID)
-
         def interleave(copy, dst, src):
             copy(
                 out=dst.rearrange("p (c i) j -> p c j i", i=RUN),
                 in_=src.rearrange("p j (c i) -> p c j i", i=RUN),
             )
-
-        def interleave_x(s):
-            interleave(nc.scalar.copy, x_bf[s][:, VEC_COLS[s] :, :], x_raw[s][:, :, VEC_COLS[s] :])
-            interleave(nc.vector.tensor_copy, x_bf[s][:, : VEC_COLS[s], :], x_raw[s][:, :, : VEC_COLS[s]])
 
         def quantize_x(s):
             nc.vector.quantize_mx(
@@ -111,7 +101,7 @@ def tile_rows_glin_sigmoid_bias_res_kernel(tc, x, w, b, r, out):
                 nc.sync.dma_start(out=out[first:last].rearrange("g m n -> m g n"), in_=y[first][:])
 
         for s in range(SETS):
-            interleave_x(s)
+            interleave(nc.vector.tensor_copy, x_bf[s][:], x_raw[s][:])
             interleave(nc.vector.tensor_copy, w_bf[s][:], w_raw[s][:])
             quantize_x(s)
             quantize_w(s)

@@ -19,8 +19,9 @@ ROWS = D // PACK
 SIDE = P // ROWS
 SETS = G // SIDE
 RUN = 2
+DMA_ALIGN = 512
 LOADS = ((0, 2), (2, 4), (4, 6), (6, 8))
-STORES = ((0, 2), (2, 4), (4, 6), (6, 8))
+STORES = tuple((g, g + 1) for g in range(G))
 
 
 def tile_rows_glin_sigmoid_bias_res_kernel(tc, x, w, b, r, out):
@@ -30,19 +31,19 @@ def tile_rows_glin_sigmoid_bias_res_kernel(tc, x, w, b, r, out):
         ps = ctx.enter_context(tc.psum_pool(name="ps", bufs=1))
         ctx.enter_context(tc.manual_schedule())
 
-        x_raw = [sb.tile([P, PACK, N], F32, name="x_raw%d" % s) for s in range(SETS)]
+        x_raw = [sb.tile([P, PACK, N], F32, name="x_raw%d" % s, align_bytes=DMA_ALIGN) for s in range(SETS)]
         x_bf = [sb.tile([P, N, PACK], BF16, name="x_bf%d" % s, align_bytes=64) for s in range(SETS)]
         x_codes = [sb.tile([P, N], U32, name="x_codes%d" % s, align_bytes=64) for s in range(SETS)]
         x_scales = [sb.tile([P, N], U8, name="x_scales%d" % s, align_bytes=64) for s in range(SETS)]
-        w_raw = [sb.tile([P, PACK, M], F32, name="w_raw%d" % s) for s in range(SETS)]
+        w_raw = [sb.tile([P, PACK, M], F32, name="w_raw%d" % s, align_bytes=DMA_ALIGN) for s in range(SETS)]
         w_bf = [sb.tile([P, M, PACK], BF16, name="w_bf%d" % s, align_bytes=64) for s in range(SETS)]
         w_codes = [sb.tile([P, M], U32, name="w_codes%d" % s, align_bytes=64) for s in range(SETS)]
         w_scales = [sb.tile([P, M], U8, name="w_scales%d" % s, align_bytes=64) for s in range(SETS)]
         b_rows = sb.tile([P, 32], F32, name="b_rows", align_bytes=64)
         b_cols = sb.tile([P, 32], F32, name="b_cols", align_bytes=64)
-        res = {first: sb.tile([P, last - first, N], F32, name="res%d" % first) for first, last in LOADS}
+        res = {first: sb.tile([P, last - first, N], F32, name="res%d" % first, align_bytes=DMA_ALIGN) for first, last in LOADS}
         act = [sb.tile([P, N], F32, name="act%d" % g) for g in range(G)]
-        y = {first: sb.tile([P, last - first, N], F32, name="y%d" % first) for first, last in STORES}
+        y = {first: sb.tile([P, last - first, N], F32, name="y%d" % first, align_bytes=DMA_ALIGN) for first, last in STORES}
         acc = [ps.tile([P, N], F32, name="acc%d" % g) for g in range(G)]
 
         x_rows = x.rearrange("g d n -> (g d) n").rearrange("(s p j) n -> s p j n", s=SETS, j=PACK)

@@ -49,10 +49,10 @@ def tile_rows_glin_sigmoid_bias_res_kernel(tc, x, w, b, r, out):
         x_rows = x.rearrange("g d n -> (g d) n").rearrange("(s p j) n -> s p j n", s=SETS, j=PACK)
         w_rows = w.rearrange("g d m -> (g d) m").rearrange("(s p j) m -> s p j m", s=SETS, j=PACK)
 
-        nc.vector.memset(b_rows[:], 0.0)
+        nc.gpsimd.memset(b_rows[:], 0.0)
         nc.sync.dma_start(out=x_raw[0][:], in_=x_rows[0])
         nc.sync.dma_start(out=w_raw[0][:], in_=w_rows[0])
-        nc.sync.dma_start(out=b_rows[0:P:4, :], in_=b.rearrange("g (q i) o -> q g (i o)", q=4))
+        nc.gpsimd.dma_start(out=b_rows[0:P:4, :], in_=b.rearrange("g (q i) o -> q g (i o)", q=4))
         nc.sync.dma_start(out=x_raw[1][:], in_=x_rows[1])
         nc.sync.dma_start(out=w_raw[1][:], in_=w_rows[1])
         for first, last in LOADS:

@@ -20,8 +20,11 @@ SIDE = P // ROWS
 SETS = G // SIDE
 RUN = 2
 DMA_ALIGN = 512
-LOADS = ((0, 2), (2, 4), (4, 6), (6, 8))
-STORES = tuple((g, g + 1) for g in range(G))
+LONE = (0, 1, 2)
+JOINED = (3,)
+LOADS = ((0, 2), (2, 3), (4, 6), (6, 7))
+HALF = N // 2
+VECTOR_COLS = (HALF, 336)
 
 
 def tile_rows_glin_sigmoid_bias_res_kernel(tc, x, w, b, r, out):
@@ -35,28 +38,45 @@ def tile_rows_glin_sigmoid_bias_res_kernel(tc, x, w, b, r, out):
         x_bf = [sb.tile([P, N, PACK], BF16, name="x_bf%d" % s, align_bytes=64) for s in range(SETS)]
         x_codes = [sb.tile([P, N], U32, name="x_codes%d" % s, align_bytes=64) for s in range(SETS)]
         x_scales = [sb.tile([P, N], U8, name="x_scales%d" % s, align_bytes=64) for s in range(SETS)]
-        w_raw = [sb.tile([P, PACK, M], F32, name="w_raw%d" % s, align_bytes=DMA_ALIGN) for s in range(SETS)]
-        w_bf = [sb.tile([P, M, PACK], BF16, name="w_bf%d" % s, align_bytes=64) for s in range(SETS)]
+        w_raw = sb.tile([P, SETS, PACK * M], F32, name="w_raw", align_bytes=DMA_ALIGN)
+        w_bf = sb.tile([P, 3 * M * PACK], BF16, name="w_bf", align_bytes=64)
         w_codes = [sb.tile([P, M], U32, name="w_codes%d" % s, align_bytes=64) for s in range(SETS)]
         w_scales = [sb.tile([P, M], U8, name="w_scales%d" % s, align_bytes=64) for s in range(SETS)]
-        b_rows = sb.tile([P, 32], F32, name="b_rows", align_bytes=64)
-        b_cols = sb.tile([P, 32], F32, name="b_cols", align_bytes=64)
-        res = {first: sb.tile([P, last - first, N], F32, name="res%d" % first, align_bytes=DMA_ALIGN) for first, last in LOADS}
-        act = [sb.tile([P, N], F32, name="act%d" % g) for g in range(G)]
-        y = {first: sb.tile([P, last - first, N], F32, name="y%d" % first, align_bytes=DMA_ALIGN) for first, last in STORES}
-        acc = [ps.tile([P, N], F32, name="acc%d" % g) for g in range(G)]
+        z_bf = [sb.tile([P, 2 * M * PACK], BF16, name="z_bf%d" % s, align_bytes=64) for s in range(SETS)]
+        z_codes = [sb.tile([P, 2 * M], U32, name="z_codes%d" % s, align_bytes=64) for s in range(SETS)]
+        z_scales = [sb.tile([P, 2 * M], U8, name="z_scales%d" % s, align_bytes=64) for s in range(SETS)]
+        b_rows = sb.tile([P, G * 32], F32, name="b_rows", align_bytes=256)
+        b_cols = sb.tile([P, G * 32], F32, name="b_cols", align_bytes=64)
+        bz_rows = sb.tile([P, 2, 32], F32, name="bz_rows", align_bytes=64)
+        bz_cols = [sb.tile([P, 32], F32, name="bz_cols%d" % k, align_bytes=64) for k in range(2)]
+        warm = sb.tile([P, 8], F32, name="warm")
+        res_lone = {first: sb.tile([P, last - first, N], F32, name="res_lone%d" % first, align_bytes=DMA_ALIGN) for first, last in LOADS}
+        res_join = {c: sb.tile([P, 2 * N], F32, name="res_join%d" % c, align_bytes=DMA_ALIGN) for c in JOINED}
+        act = {(c, k): sb.tile([P, N], F32, name="act%d%d" % (c, k)) for c in range(SIDE) for k in range(2)}
+        y_lone = {(c, s): sb.tile([P, N], F32, name="y_lone%d%d" % (c, s), align_bytes=DMA_ALIGN) for c in LONE for s in range(SETS)}
+        y_join = {c: sb.tile([P, 2 * N], F32, name="y_join%d" % c, align_bytes=DMA_ALIGN) for c in JOINED}
+        acc = {(c, k): ps.tile([P, N], F32, name="acc%d%d" % (c, k)) for c in range(SIDE) for k in range(2)}
 
         x_rows = x.rearrange("g d n -> (g d) n").rearrange("(s p j) n -> s p j n", s=SETS, j=PACK)
-        w_rows = w.rearrange("g d m -> (g d) m").rearrange("(s p j) m -> s p j m", s=SETS, j=PACK)
+        w_rows = w.rearrange("g d m -> (g d) m").rearrange("(s p j) m -> p s (j m)", s=SETS, j=PACK)
+
+        def paired(t, c):
+            return t.rearrange("(h c) (q k) n -> c q h (k n)", h=SETS, k=2)[c]
 
         nc.gpsimd.memset(b_rows[:], 0.0)
-        nc.sync.dma_start(out=x_raw[0][:], in_=x_rows[0])
-        nc.sync.dma_start(out=w_raw[0][:], in_=w_rows[0])
-        nc.gpsimd.dma_start(out=b_rows[0:P:4, :], in_=b.rearrange("g (q i) o -> q g (i o)", q=4))
-        nc.sync.dma_start(out=x_raw[1][:], in_=x_rows[1])
-        nc.sync.dma_start(out=w_raw[1][:], in_=w_rows[1])
+        nc.vector.memset(w_bf[:, M * PACK : 2 * M * PACK], 0.0)
+        nc.scalar.activation(out=warm[:, 0:1], in_=w_bf[:, M * PACK : M * PACK + 1], func=SIGMOID)
+        nc.sync.dma_start(out=w_raw[:], in_=w_rows)
+        nc.sync.dma_start(
+            out=b_rows[0:P:32, :].rearrange("q (g i) -> q g i", g=G),
+            in_=b.rearrange("g (q i) o -> q g (i o)", q=4),
+        )
+        for s in range(SETS):
+            nc.sync.dma_start(out=x_raw[s][:], in_=x_rows[s])
         for first, last in LOADS:
-            nc.sync.dma_start(out=res[first][:], in_=r[first:last].rearrange("g m n -> m g n"))
+            nc.sync.dma_start(out=res_lone[first][:], in_=r[first:last].rearrange("g m n -> m g n"))
+        for c in JOINED:
+            nc.sync.dma_start(out=res_join[c][:], in_=paired(r, c))
 
         def interleave(copy, dst, src):
             copy(
@@ -64,51 +84,92 @@ def tile_rows_glin_sigmoid_bias_res_kernel(tc, x, w, b, r, out):
                 in_=src.rearrange("p j (c i) -> p c j i", i=RUN),
             )
 
-        def quantize_x(s):
-            nc.vector.quantize_mx(
-                out=x_codes[s][:].bitcast(FP8X4),
-                scales=x_scales[s][:],
-                in_=x_bf[s][:].rearrange("p n j -> p (n j)"),
+        def quantize(codes, scales, values):
+            nc.vector.quantize_mx(out=codes.bitcast(FP8X4), scales=scales, in_=values)
+
+        def w_slot(s):
+            return w_bf[:, 2 * s * M * PACK : (2 * s + 1) * M * PACK]
+
+        def round_w(s):
+            interleave(
+                nc.scalar.copy,
+                w_slot(s).rearrange("p (m j) -> p m j", j=PACK),
+                w_raw[:, s, :].rearrange("p (j m) -> p j m", j=PACK),
             )
 
-        def quantize_w(s):
-            nc.vector.quantize_mx(
-                out=w_codes[s][:].bitcast(FP8X4),
-                scales=w_scales[s][:],
-                in_=w_bf[s][:].rearrange("p m j -> p (m j)"),
+        def deal_w(s):
+            nc.vector.tensor_copy(
+                out=z_bf[s][:].rearrange("p (k q h j) -> p k q h j", k=2, h=2, j=PACK),
+                in_=w_bf[:, s * M * PACK : (s + 2) * M * PACK].rearrange("p (h q k j) -> p k q h j", h=2, k=2, j=PACK),
             )
 
-        def multiply(s):
-            for c in range(SIDE):
-                rows = slice(ROWS * c, ROWS * (c + 1))
-                nc.tensor.matmul_mx(
-                    out=acc[SIDE * s + c][:],
-                    lhsT=w_codes[s][rows, :].bitcast(FP8X4),
-                    lhsT_scale=w_scales[s][rows, :],
-                    rhs=x_codes[s][rows, :].bitcast(FP8X4),
-                    rhs_scale=x_scales[s][rows, :],
-                    start=True,
-                    stop=True,
-                )
+        def multiply(c, k, s):
+            rows = slice(ROWS * c, ROWS * (c + 1))
+            lone = c in LONE
+            codes = w_codes[s][rows, :] if lone else z_codes[s][rows, M * k : M * (k + 1)]
+            scales = w_scales[s][rows, :] if lone else z_scales[s][rows, M * k : M * (k + 1)]
+            nc.tensor.matmul_mx(
+                out=acc[c, k][:],
+                lhsT=codes.bitcast(FP8X4),
+                lhsT_scale=scales,
+                rhs=x_codes[s][rows, :].bitcast(FP8X4),
+                rhs_scale=x_scales[s][rows, :],
+                start=lone or s == 0,
+                stop=lone or s == 1,
+            )
 
-        def activate(g):
-            nc.scalar.activation(out=act[g][:], in_=acc[g][:], func=SIGMOID, bias=b_cols[:, 4 * g : 4 * g + 1])
+        def prepare_x(s):
+            cut = VECTOR_COLS[s]
+            interleave(nc.scalar.copy, x_bf[s][:, cut:, :], x_raw[s][:, :, cut:])
+            for first in range(0, cut, HALF):
+                last = min(first + HALF, cut)
+                interleave(nc.vector.tensor_copy, x_bf[s][:, first:last, :], x_raw[s][:, :, first:last])
+            for first in (0, HALF):
+                cols = slice(first, first + HALF)
+                quantize(x_codes[s][:, cols], x_scales[s][:, cols], x_bf[s][:, cols, :].rearrange("p n j -> p (n j)"))
 
-        def finish(g):
-            first, last = [span for span in STORES if span[0] <= g < span[1]][0]
-            start = [span[0] for span in LOADS if span[0] <= g < span[1]][0]
-            nc.vector.tensor_tensor(out=y[first][:, g - first, :], in0=act[g][:], in1=res[start][:, g - start, :], op=ADD)
-            if g == last - 1:
-                nc.sync.dma_start(out=out[first:last].rearrange("g m n -> m g n"), in_=y[first][:])
+        def finish(c, k):
+            lone = c in LONE
+            if lone:
+                col = 32 * (SIDE * k + c)
+                bias = b_cols[:, col : col + 1]
+                g = SIDE * k + c
+                start = [first for first, last in LOADS if first <= g < last][0]
+                residual, result = res_lone[start][:, g - start, :], y_lone[c, k][:]
+            else:
+                bias = bz_cols[k][:, 0:1]
+                residual, result = res_join[c][:, N * k : N * (k + 1)], y_join[c][:, N * k : N * (k + 1)]
+            width = HALF if not lone and k == 1 else N
+            for first in range(0, N, width):
+                cols = slice(first, first + width)
+                nc.scalar.activation(out=act[c, k][:, cols], in_=acc[c, k][:, cols], func=SIGMOID, bias=bias)
+                nc.vector.tensor_tensor(out=result[:, cols], in0=act[c, k][:, cols], in1=residual[:, cols], op=ADD)
+            if lone:
+                nc.sync.dma_start(out=out[SIDE * k + c], in_=result)
+            elif k == 1:
+                nc.sync.dma_start(out=paired(out, c), in_=y_join[c][:])
 
+        nc.vector.tensor_copy(
+            out=bz_rows[:].rearrange("p k (q h) -> p k q h", h=2),
+            in_=b_rows[:].rearrange("p (h c q k) -> p c k q h", h=2, c=SIDE, k=2)[:, JOINED[0]],
+        )
+        nc.vector.transpose(out=b_cols[:], in_=b_rows[:])
+        for k in range(2):
+            nc.vector.transpose(out=bz_cols[k][:], in_=bz_rows[:, k, :])
         for s in range(SETS):
-            interleave(nc.vector.tensor_copy, x_bf[s][:], x_raw[s][:])
-            interleave(nc.vector.tensor_copy, w_bf[s][:], w_raw[s][:])
-            quantize_x(s)
-            quantize_w(s)
-            multiply(s)
-            if s == 0:
-                nc.vector.transpose(out=b_cols[:], in_=b_rows[:])
-        for g in range(G):
-            activate(g)
-            finish(g)
+            round_w(s)
+        for s in range(SETS):
+            deal_w(s)
+            quantize(w_codes[s][:], w_scales[s][:], w_slot(s))
+        for s in range(SETS):
+            quantize(z_codes[s][:], z_scales[s][:], z_bf[s][:])
+        for s in range(SETS):
+            prepare_x(s)
+            for c in range(SIDE):
+                multiply(c, s if c in LONE else 0, s)
+            for c in JOINED:
+                multiply(c, 1, s)
+
+        banks = [(c, s) for s in range(SETS) for c in LONE] + [(c, k) for c in JOINED for k in range(2)]
+        for c, k in banks:
+            finish(c, k)

@@ -19,12 +19,13 @@ ROWS = D // PACK
 SIDE = P // ROWS
 SETS = G // SIDE
 RUN = 2
+QUAD = 32
 DMA_ALIGN = 512
-LONE = (0, 1, 2)
-JOINED = (3,)
-LOADS = ((0, 2), (2, 3), (4, 6), (6, 7))
+JOINED = SIDE - 1
+LONE = tuple(range(JOINED))
 HALF = N // 2
-VECTOR_COLS = (HALF, 336)
+VECTOR_COLS = 288
+W_SLOT = M * PACK
 
 
 def tile_rows_glin_sigmoid_bias_res_kernel(tc, x, w, b, r, out):
@@ -34,49 +35,52 @@ def tile_rows_glin_sigmoid_bias_res_kernel(tc, x, w, b, r, out):
         ps = ctx.enter_context(tc.psum_pool(name="ps", bufs=1))
         ctx.enter_context(tc.manual_schedule())
 
+        banks = [(c, s) for s in range(SETS) for c in LONE] + [(JOINED, k) for k in range(2)]
+        lone_groups = [SIDE * s + c for s in range(SETS) for c in LONE]
+        res_loads = [lone_groups[i : i + 2] for i in range(0, len(lone_groups), 2)]
+
         x_raw = [sb.tile([P, PACK, N], F32, name="x_raw%d" % s, align_bytes=DMA_ALIGN) for s in range(SETS)]
         x_bf = [sb.tile([P, N, PACK], BF16, name="x_bf%d" % s, align_bytes=64) for s in range(SETS)]
         x_codes = [sb.tile([P, N], U32, name="x_codes%d" % s, align_bytes=64) for s in range(SETS)]
         x_scales = [sb.tile([P, N], U8, name="x_scales%d" % s, align_bytes=64) for s in range(SETS)]
-        w_raw = sb.tile([P, SETS, PACK * M], F32, name="w_raw", align_bytes=DMA_ALIGN)
-        w_bf = sb.tile([P, 3 * M * PACK], BF16, name="w_bf", align_bytes=64)
+        w_raw = [sb.tile([P, PACK, M], F32, name="w_raw%d" % s, align_bytes=DMA_ALIGN) for s in range(SETS)]
+        w_bf = sb.tile([P, 3 * W_SLOT], BF16, name="w_bf", align_bytes=64)
         w_codes = [sb.tile([P, M], U32, name="w_codes%d" % s, align_bytes=64) for s in range(SETS)]
         w_scales = [sb.tile([P, M], U8, name="w_scales%d" % s, align_bytes=64) for s in range(SETS)]
-        z_bf = [sb.tile([P, 2 * M * PACK], BF16, name="z_bf%d" % s, align_bytes=64) for s in range(SETS)]
+        z_bf = [sb.tile([P, 2 * W_SLOT], BF16, name="z_bf%d" % s, align_bytes=64) for s in range(SETS)]
         z_codes = [sb.tile([P, 2 * M], U32, name="z_codes%d" % s, align_bytes=64) for s in range(SETS)]
         z_scales = [sb.tile([P, 2 * M], U8, name="z_scales%d" % s, align_bytes=64) for s in range(SETS)]
-        b_rows = sb.tile([P, G * 32], F32, name="b_rows", align_bytes=256)
-        b_cols = sb.tile([P, G * 32], F32, name="b_cols", align_bytes=64)
-        bz_rows = sb.tile([P, 2, 32], F32, name="bz_rows", align_bytes=64)
-        bz_cols = [sb.tile([P, 32], F32, name="bz_cols%d" % k, align_bytes=64) for k in range(2)]
+        b_raw = sb.tile([P, G * QUAD], F32, name="b_raw", align_bytes=256)
+        b_rows = sb.tile([P, G * QUAD], F32, name="b_rows", align_bytes=64)
+        b_cols = sb.tile([P, G * QUAD], F32, name="b_cols", align_bytes=64)
         warm = sb.tile([P, 8], F32, name="warm")
-        res_lone = {first: sb.tile([P, last - first, N], F32, name="res_lone%d" % first, align_bytes=DMA_ALIGN) for first, last in LOADS}
-        res_join = {c: sb.tile([P, 2 * N], F32, name="res_join%d" % c, align_bytes=DMA_ALIGN) for c in JOINED}
-        act = {(c, k): sb.tile([P, N], F32, name="act%d%d" % (c, k)) for c in range(SIDE) for k in range(2)}
-        y_lone = {(c, s): sb.tile([P, N], F32, name="y_lone%d%d" % (c, s), align_bytes=DMA_ALIGN) for c in LONE for s in range(SETS)}
-        y_join = {c: sb.tile([P, 2 * N], F32, name="y_join%d" % c, align_bytes=DMA_ALIGN) for c in JOINED}
-        acc = {(c, k): ps.tile([P, N], F32, name="acc%d%d" % (c, k)) for c in range(SIDE) for k in range(2)}
+        res = {pair[0]: sb.tile([P, 2, N], F32, name="res%d" % pair[0], align_bytes=DMA_ALIGN) for pair in res_loads}
+        res_joined = sb.tile([P, 2, N], F32, name="res_joined", align_bytes=DMA_ALIGN)
+        act = {bank: sb.tile([P, N], F32, name="act%d%d" % bank) for bank in banks}
+        y = {g: sb.tile([P, N], F32, name="y%d" % g, align_bytes=DMA_ALIGN) for g in lone_groups}
+        y_joined = sb.tile([P, 2, N], F32, name="y_joined", align_bytes=DMA_ALIGN)
+        acc = {bank: ps.tile([P, N], F32, name="acc%d%d" % bank) for bank in banks}
 
         x_rows = x.rearrange("g d n -> (g d) n").rearrange("(s p j) n -> s p j n", s=SETS, j=PACK)
-        w_rows = w.rearrange("g d m -> (g d) m").rearrange("(s p j) m -> p s (j m)", s=SETS, j=PACK)
+        w_rows = w.rearrange("g d m -> (g d) m").rearrange("(s p j) m -> s p j m", s=SETS, j=PACK)
 
-        def paired(t, c):
-            return t.rearrange("(h c) (q k) n -> c q h (k n)", h=SETS, k=2)[c]
+        def joined_rows(t):
+            return t.rearrange("(s c) (q k) n -> c q s (k n)", s=SETS, k=2)[JOINED]
 
-        nc.gpsimd.memset(b_rows[:], 0.0)
-        nc.vector.memset(w_bf[:, M * PACK : 2 * M * PACK], 0.0)
-        nc.scalar.activation(out=warm[:, 0:1], in_=w_bf[:, M * PACK : M * PACK + 1], func=SIGMOID)
-        nc.sync.dma_start(out=w_raw[:], in_=w_rows)
+        nc.gpsimd.memset(b_raw[:], 0.0)
+        nc.vector.memset(w_bf[:, W_SLOT : 2 * W_SLOT], 0.0)
+        nc.scalar.activation(out=warm[:, 0:1], in_=w_bf[:, W_SLOT : W_SLOT + 1], func=SIGMOID)
+        nc.sync.dma_start(out=x_raw[0][:], in_=x_rows[0])
         nc.sync.dma_start(
-            out=b_rows[0:P:32, :].rearrange("q (g i) -> q g i", g=G),
-            in_=b.rearrange("g (q i) o -> q g (i o)", q=4),
+            out=b_raw[0:P:QUAD, :].rearrange("q (g i) -> q g i", g=G),
+            in_=b.rearrange("g (q i) o -> q g (i o)", i=QUAD),
         )
-        for s in range(SETS):
-            nc.sync.dma_start(out=x_raw[s][:], in_=x_rows[s])
-        for first, last in LOADS:
-            nc.sync.dma_start(out=res_lone[first][:], in_=r[first:last].rearrange("g m n -> m g n"))
-        for c in JOINED:
-            nc.sync.dma_start(out=res_join[c][:], in_=paired(r, c))
+        nc.sync.dma_start(out=w_raw[0][:], in_=w_rows[0])
+        nc.sync.dma_start(out=x_raw[1][:], in_=x_rows[1])
+        nc.sync.dma_start(out=w_raw[1][:], in_=w_rows[1])
+        for first, second in res_loads:
+            nc.sync.dma_start(out=res[first][:], in_=r[first : second + 1 : second - first].rearrange("g m n -> m g n"))
+        nc.sync.dma_start(out=res_joined[:].rearrange("p k n -> p (k n)"), in_=joined_rows(r))
 
         def interleave(copy, dst, src):
             copy(
@@ -87,21 +91,9 @@ def tile_rows_glin_sigmoid_bias_res_kernel(tc, x, w, b, r, out):
         def quantize(codes, scales, values):
             nc.vector.quantize_mx(out=codes.bitcast(FP8X4), scales=scales, in_=values)
 
-        def w_slot(s):
-            return w_bf[:, 2 * s * M * PACK : (2 * s + 1) * M * PACK]
-
-        def round_w(s):
-            interleave(
-                nc.scalar.copy,
-                w_slot(s).rearrange("p (m j) -> p m j", j=PACK),
-                w_raw[:, s, :].rearrange("p (j m) -> p j m", j=PACK),
-            )
-
-        def deal_w(s):
-            nc.vector.tensor_copy(
-                out=z_bf[s][:].rearrange("p (k q h j) -> p k q h j", k=2, h=2, j=PACK),
-                in_=w_bf[:, s * M * PACK : (s + 2) * M * PACK].rearrange("p (h q k j) -> p k q h j", h=2, k=2, j=PACK),
-            )
+        def quantize_x(s, half):
+            cols = slice(HALF * half, HALF * (half + 1))
+            quantize(x_codes[s][:, cols], x_scales[s][:, cols], x_bf[s][:, cols, :].rearrange("p n j -> p (n j)"))
 
         def multiply(c, k, s):
             rows = slice(ROWS * c, ROWS * (c + 1))
@@ -115,61 +107,57 @@ def tile_rows_glin_sigmoid_bias_res_kernel(tc, x, w, b, r, out):
                 rhs=x_codes[s][rows, :].bitcast(FP8X4),
                 rhs_scale=x_scales[s][rows, :],
                 start=lone or s == 0,
-                stop=lone or s == 1,
+                stop=lone or s == SETS - 1,
             )
 
-        def prepare_x(s):
-            cut = VECTOR_COLS[s]
-            interleave(nc.scalar.copy, x_bf[s][:, cut:, :], x_raw[s][:, :, cut:])
-            for first in range(0, cut, HALF):
-                last = min(first + HALF, cut)
-                interleave(nc.vector.tensor_copy, x_bf[s][:, first:last, :], x_raw[s][:, :, first:last])
-            for first in (0, HALF):
-                cols = slice(first, first + HALF)
-                quantize(x_codes[s][:, cols], x_scales[s][:, cols], x_bf[s][:, cols, :].rearrange("p n j -> p (n j)"))
+        def turn_bias():
+            raw = b_raw[:].rearrange("p (s c i) -> p s c i", s=SETS, c=SIDE)
+            rows = b_rows[:].rearrange("p (k c i) -> p k c i", k=2, c=SIDE)
+            nc.scalar.copy(out=rows[:, :, :JOINED, :], in_=raw[:, :, :JOINED, :])
+            nc.scalar.copy(
+                out=rows[:, :, JOINED, :].rearrange("p k (q s) -> p k q s", s=SETS),
+                in_=raw[:, :, JOINED, :].rearrange("p s (q k) -> p k q s", k=2),
+            )
+            nc.vector.transpose(out=b_cols[:], in_=b_rows[:])
 
         def finish(c, k):
-            lone = c in LONE
-            if lone:
-                col = 32 * (SIDE * k + c)
-                bias = b_cols[:, col : col + 1]
+            col = QUAD * (SIDE * k + c)
+            if c in LONE:
                 g = SIDE * k + c
-                start = [first for first, last in LOADS if first <= g < last][0]
-                residual, result = res_lone[start][:, g - start, :], y_lone[c, k][:]
+                pair = res_loads[lone_groups.index(g) // 2]
+                residual, result = res[pair[0]][:, pair.index(g), :], y[g][:]
             else:
-                bias = bz_cols[k][:, 0:1]
-                residual, result = res_join[c][:, N * k : N * (k + 1)], y_join[c][:, N * k : N * (k + 1)]
-            width = HALF if not lone and k == 1 else N
+                residual, result = res_joined[:, k, :], y_joined[:, k, :]
+            width = HALF if (c, k) == banks[-1] else N
             for first in range(0, N, width):
                 cols = slice(first, first + width)
-                nc.scalar.activation(out=act[c, k][:, cols], in_=acc[c, k][:, cols], func=SIGMOID, bias=bias)
+                nc.scalar.activation(out=act[c, k][:, cols], in_=acc[c, k][:, cols], func=SIGMOID, bias=b_cols[:, col : col + 1])
                 nc.vector.tensor_tensor(out=result[:, cols], in0=act[c, k][:, cols], in1=residual[:, cols], op=ADD)
-            if lone:
-                nc.sync.dma_start(out=out[SIDE * k + c], in_=result)
+            if c in LONE:
+                nc.sync.dma_start(out=out[g], in_=result)
             elif k == 1:
-                nc.sync.dma_start(out=paired(out, c), in_=y_join[c][:])
+                nc.sync.dma_start(out=joined_rows(out), in_=y_joined[:].rearrange("p k n -> p (k n)"))
 
-        nc.vector.tensor_copy(
-            out=bz_rows[:].rearrange("p k (q h) -> p k q h", h=2),
-            in_=b_rows[:].rearrange("p (h c q k) -> p c k q h", h=2, c=SIDE, k=2)[:, JOINED[0]],
-        )
-        nc.vector.transpose(out=b_cols[:], in_=b_rows[:])
-        for k in range(2):
-            nc.vector.transpose(out=bz_cols[k][:], in_=bz_rows[:, k, :])
         for s in range(SETS):
-            round_w(s)
-        for s in range(SETS):
-            deal_w(s)
-            quantize(w_codes[s][:], w_scales[s][:], w_slot(s))
-        for s in range(SETS):
+            w_slot = w_bf[:, 2 * s * W_SLOT : (2 * s + 1) * W_SLOT]
+            interleave(nc.scalar.copy, x_bf[s][:, VECTOR_COLS:, :], x_raw[s][:, :, VECTOR_COLS:])
+            interleave(nc.vector.tensor_copy, x_bf[s][:, :VECTOR_COLS, :], x_raw[s][:, :, :VECTOR_COLS])
+            interleave(nc.vector.tensor_copy, w_slot.rearrange("p (m j) -> p m j", j=PACK), w_raw[s][:])
+            quantize_x(s, 0)
+            quantize(w_codes[s][:], w_scales[s][:], w_slot)
+            quantize_x(s, 1)
+            for c in LONE:
+                multiply(c, s, s)
+            nc.vector.tensor_copy(
+                out=z_bf[s][:].rearrange("p (k q h j) -> p k q h j", k=2, h=SETS, j=PACK),
+                in_=w_bf[:, s * W_SLOT : (s + 2) * W_SLOT].rearrange("p (h q k j) -> p k q h j", h=SETS, k=2, j=PACK),
+            )
+            if s == 0:
+                turn_bias()
+            else:
+                finish(*banks[0])
             quantize(z_codes[s][:], z_scales[s][:], z_bf[s][:])
-        for s in range(SETS):
-            prepare_x(s)
-            for c in range(SIDE):
-                multiply(c, s if c in LONE else 0, s)
-            for c in JOINED:
-                multiply(c, 1, s)
-
-        banks = [(c, s) for s in range(SETS) for c in LONE] + [(c, k) for c in JOINED for k in range(2)]
-        for c, k in banks:
+            for k in range(2):
+                multiply(JOINED, k, s)
+        for c, k in banks[1:]:
             finish(c, k)

@@ -68,8 +68,9 @@ def tile_rows_glin_sigmoid_bias_res_kernel(tc, x, w, b, r, out):
             return t.rearrange("(s c) (q k) n -> c q s (k n)", s=SETS, k=2)[JOINED]
 
         nc.gpsimd.memset(b_raw[:], 0.0)
+        nc.vector.memset(warm[:, 0:1], 0.0)
         nc.vector.memset(w_bf[:, W_SLOT : 2 * W_SLOT], 0.0)
-        nc.scalar.activation(out=warm[:, 0:1], in_=w_bf[:, W_SLOT : W_SLOT + 1], func=SIGMOID)
+        nc.scalar.activation(out=warm[:, 1:2], in_=warm[:, 0:1], func=SIGMOID)
         nc.sync.dma_start(out=x_raw[0][:], in_=x_rows[0])
         nc.sync.dma_start(
             out=b_raw[0:P:QUAD, :].rearrange("q (g i) -> q g i", g=G),
@@ -128,11 +129,8 @@ def tile_rows_glin_sigmoid_bias_res_kernel(tc, x, w, b, r, out):
                 residual, result = res[pair[0]][:, pair.index(g), :], y[g][:]
             else:
                 residual, result = res_joined[:, k, :], y_joined[:, k, :]
-            width = HALF if (c, k) == banks[-1] else N
-            for first in range(0, N, width):
-                cols = slice(first, first + width)
-                nc.scalar.activation(out=act[c, k][:, cols], in_=acc[c, k][:, cols], func=SIGMOID, bias=b_cols[:, col : col + 1])
-                nc.vector.tensor_tensor(out=result[:, cols], in0=act[c, k][:, cols], in1=residual[:, cols], op=ADD)
+            nc.scalar.activation(out=act[c, k][:], in_=acc[c, k][:], func=SIGMOID, bias=b_cols[:, col : col + 1])
+            nc.vector.tensor_tensor(out=result, in0=act[c, k][:], in1=residual, op=ADD)
             if c in LONE:
                 nc.sync.dma_start(out=out[g], in_=result)
             elif k == 1:

from contextlib import ExitStack

import concourse.mybir as mybir

G, D, M, N = 8, 128, 128, 512
FLOPS = 2 * G * D * M * N

F32 = mybir.dt.float32
BF16 = mybir.dt.bfloat16
U32 = mybir.dt.uint32
U8 = mybir.dt.uint8
FP8X4 = mybir.dt.float8_e4m3fn_x4
SIGMOID = mybir.ActivationFunctionType.Sigmoid
ADD = mybir.AluOpType.add

P = 128
PACK = 4
ROWS = D // PACK
SIDE = P // ROWS
SETS = G // SIDE
RUN = 2
QUAD = 32
DMA_ALIGN = 512
JOINED = SIDE - 1
LONE = tuple(range(JOINED))
HALF = N // 2
VECTOR_COLS = 288
W_SLOT = M * PACK


def tile_rows_glin_sigmoid_bias_res_kernel(tc, x, w, b, r, out):
    nc = tc.nc
    with ExitStack() as ctx:
        sb = ctx.enter_context(tc.tile_pool(name="sb", bufs=1))
        ps = ctx.enter_context(tc.psum_pool(name="ps", bufs=1))
        ctx.enter_context(tc.manual_schedule())

        banks = [(c, s) for s in range(SETS) for c in LONE] + [(JOINED, k) for k in range(2)]
        lone_groups = [SIDE * s + c for s in range(SETS) for c in LONE]
        res_loads = [lone_groups[i : i + 2] for i in range(0, len(lone_groups), 2)]

        x_raw = [sb.tile([P, PACK, N], F32, name="x_raw%d" % s, align_bytes=DMA_ALIGN) for s in range(SETS)]
        x_bf = [sb.tile([P, N, PACK], BF16, name="x_bf%d" % s, align_bytes=64) for s in range(SETS)]
        x_codes = [sb.tile([P, N], U32, name="x_codes%d" % s, align_bytes=64) for s in range(SETS)]
        x_scales = [sb.tile([P, N], U8, name="x_scales%d" % s, align_bytes=64) for s in range(SETS)]
        w_raw = [sb.tile([P, PACK, M], F32, name="w_raw%d" % s, align_bytes=DMA_ALIGN) for s in range(SETS)]
        w_bf = sb.tile([P, 3 * W_SLOT], BF16, name="w_bf", align_bytes=64)
        w_codes = [sb.tile([P, M], U32, name="w_codes%d" % s, align_bytes=64) for s in range(SETS)]
        w_scales = [sb.tile([P, M], U8, name="w_scales%d" % s, align_bytes=64) for s in range(SETS)]
        z_bf = [sb.tile([P, 2 * W_SLOT], BF16, name="z_bf%d" % s, align_bytes=64) for s in range(SETS)]
        z_codes = [sb.tile([P, 2 * M], U32, name="z_codes%d" % s, align_bytes=64) for s in range(SETS)]
        z_scales = [sb.tile([P, 2 * M], U8, name="z_scales%d" % s, align_bytes=64) for s in range(SETS)]
        b_raw = sb.tile([P, G * QUAD], F32, name="b_raw", align_bytes=256)
        b_rows = sb.tile([P, G * QUAD], F32, name="b_rows", align_bytes=64)
        b_cols = sb.tile([P, G * QUAD], F32, name="b_cols", align_bytes=64)
        warm = sb.tile([P, 8], F32, name="warm")
        res = {pair[0]: sb.tile([P, 2, N], F32, name="res%d" % pair[0], align_bytes=DMA_ALIGN) for pair in res_loads}
        res_joined = sb.tile([P, 2, N], F32, name="res_joined", align_bytes=DMA_ALIGN)
        act = {bank: sb.tile([P, N], F32, name="act%d%d" % bank) for bank in banks}
        y = {g: sb.tile([P, N], F32, name="y%d" % g, align_bytes=DMA_ALIGN) for g in lone_groups}
        y_joined = sb.tile([P, 2, N], F32, name="y_joined", align_bytes=DMA_ALIGN)
        acc = {bank: ps.tile([P, N], F32, name="acc%d%d" % bank) for bank in banks}

        x_rows = x.rearrange("g d n -> (g d) n").rearrange("(s p j) n -> s p j n", s=SETS, j=PACK)
        w_rows = w.rearrange("g d m -> (g d) m").rearrange("(s p j) m -> s p j m", s=SETS, j=PACK)

        def joined_rows(t):
            return t.rearrange("(s c) (q k) n -> c q s (k n)", s=SETS, k=2)[JOINED]

        nc.gpsimd.memset(b_raw[:], 0.0)
        nc.vector.memset(warm[:, 0:1], 0.0)
        nc.vector.memset(w_bf[:, W_SLOT : 2 * W_SLOT], 0.0)
        nc.scalar.activation(out=warm[:, 1:2], in_=warm[:, 0:1], func=SIGMOID)
        nc.sync.dma_start(out=x_raw[0][:], in_=x_rows[0])
        nc.sync.dma_start(
            out=b_raw[0:P:QUAD, :].rearrange("q (g i) -> q g i", g=G),
            in_=b.rearrange("g (q i) o -> q g (i o)", i=QUAD),
        )
        nc.sync.dma_start(out=w_raw[0][:], in_=w_rows[0])
        nc.sync.dma_start(out=x_raw[1][:], in_=x_rows[1])
        nc.sync.dma_start(out=w_raw[1][:], in_=w_rows[1])
        for first, second in res_loads:
            nc.sync.dma_start(out=res[first][:], in_=r[first : second + 1 : second - first].rearrange("g m n -> m g n"))
        nc.sync.dma_start(out=res_joined[:].rearrange("p k n -> p (k n)"), in_=joined_rows(r))

        def interleave(copy, dst, src):
            copy(
                out=dst.rearrange("p (c i) j -> p c j i", i=RUN),
                in_=src.rearrange("p j (c i) -> p c j i", i=RUN),
            )

        def quantize(codes, scales, values):
            nc.vector.quantize_mx(out=codes.bitcast(FP8X4), scales=scales, in_=values)

        def quantize_x(s, half):
            cols = slice(HALF * half, HALF * (half + 1))
            quantize(x_codes[s][:, cols], x_scales[s][:, cols], x_bf[s][:, cols, :].rearrange("p n j -> p (n j)"))

        def multiply(c, k, s):
            rows = slice(ROWS * c, ROWS * (c + 1))
            lone = c in LONE
            codes = w_codes[s][rows, :] if lone else z_codes[s][rows, M * k : M * (k + 1)]
            scales = w_scales[s][rows, :] if lone else z_scales[s][rows, M * k : M * (k + 1)]
            nc.tensor.matmul_mx(
                out=acc[c, k][:],
                lhsT=codes.bitcast(FP8X4),
                lhsT_scale=scales,
                rhs=x_codes[s][rows, :].bitcast(FP8X4),
                rhs_scale=x_scales[s][rows, :],
                start=lone or s == 0,
                stop=lone or s == SETS - 1,
            )

        def turn_bias():
            raw = b_raw[:].rearrange("p (s c i) -> p s c i", s=SETS, c=SIDE)
            rows = b_rows[:].rearrange("p (k c i) -> p k c i", k=2, c=SIDE)
            nc.scalar.copy(out=rows[:, :, :JOINED, :], in_=raw[:, :, :JOINED, :])
            nc.scalar.copy(
                out=rows[:, :, JOINED, :].rearrange("p k (q s) -> p k q s", s=SETS),
                in_=raw[:, :, JOINED, :].rearrange("p s (q k) -> p k q s", k=2),
            )
            nc.vector.transpose(out=b_cols[:], in_=b_rows[:])

        def finish(c, k):
            col = QUAD * (SIDE * k + c)
            if c in LONE:
                g = SIDE * k + c
                pair = res_loads[lone_groups.index(g) // 2]
                residual, result = res[pair[0]][:, pair.index(g), :], y[g][:]
            else:
                residual, result = res_joined[:, k, :], y_joined[:, k, :]
            nc.scalar.activation(out=act[c, k][:], in_=acc[c, k][:], func=SIGMOID, bias=b_cols[:, col : col + 1])
            nc.vector.tensor_tensor(out=result, in0=act[c, k][:], in1=residual, op=ADD)
            if c in LONE:
                nc.sync.dma_start(out=out[g], in_=result)
            elif k == 1:
                nc.sync.dma_start(out=joined_rows(out), in_=y_joined[:].rearrange("p k n -> p (k n)"))

        for s in range(SETS):
            w_slot = w_bf[:, 2 * s * W_SLOT : (2 * s + 1) * W_SLOT]
            interleave(nc.scalar.copy, x_bf[s][:, VECTOR_COLS:, :], x_raw[s][:, :, VECTOR_COLS:])
            interleave(nc.vector.tensor_copy, x_bf[s][:, :VECTOR_COLS, :], x_raw[s][:, :, :VECTOR_COLS])
            interleave(nc.vector.tensor_copy, w_slot.rearrange("p (m j) -> p m j", j=PACK), w_raw[s][:])
            quantize_x(s, 0)
            quantize(w_codes[s][:], w_scales[s][:], w_slot)
            quantize_x(s, 1)
            for c in LONE:
                multiply(c, s, s)
            nc.vector.tensor_copy(
                out=z_bf[s][:].rearrange("p (k q h j) -> p k q h j", k=2, h=SETS, j=PACK),
                in_=w_bf[:, s * W_SLOT : (s + 2) * W_SLOT].rearrange("p (h q k j) -> p k q h j", h=SETS, k=2, j=PACK),
            )
            if s == 0:
                turn_bias()
            else:
                finish(*banks[0])
            quantize(z_codes[s][:], z_scales[s][:], z_bf[s][:])
            for k in range(2):
                multiply(JOINED, k, s)
        for c, k in banks[1:]:
            finish(c, k)
